import numpy as np
import ml_dtypes


def mxq(x, axis, fmt="e4m3"):
    dtype, down = {"e4m3": (ml_dtypes.float8_e4m3fn, 7), "e5m2": (ml_dtypes.float8_e5m2, 14)}[fmt]
    v = np.moveaxis(np.asarray(x, np.float32).astype(ml_dtypes.bfloat16).astype(np.float64), axis, -1)
    blocks = v.reshape(v.shape[:-1] + (-1, 32))
    amax = np.abs(blocks).max(-1, keepdims=True)
    byte = np.maximum(np.where(amax > 0, np.frexp(amax)[1] - 1 + 127, 0) - down, 1)
    scale = np.exp2(byte - 127.0)
    codes = (blocks / scale).astype(np.float32).astype(dtype).astype(np.float64)
    return np.moveaxis((codes * scale).reshape(v.shape), -1, axis)


WIDE = False


def mx_kscale(k):
    if not WIDE:
        return np.ones(k)
    levels = np.array([10, -10, 5, -5, 0])
    if k % 512:
        return np.exp2(np.random.permutation(np.resize(levels, k // 32))).repeat(32)
    a = np.empty((k // 512, 16))
    for p in range(k // 512):
        a[p, :8] = np.random.permutation(np.resize(levels, 8))
        for g in range(8):
            far = levels[np.abs(levels - a[p, g]) >= 10]
            a[p, g + 8] = far[np.random.randint(len(far))]
    return np.exp2(a.ravel()).repeat(32)


BF16 = ml_dtypes.bfloat16


def bf(x):
    return np.asarray(x, np.float32).astype(BF16)


def f64(x):
    return np.asarray(x).astype(np.float64)

def planes(Y):
    n, m = Y.shape
    b = f64(bf(Y)).reshape(n // 32, 32, m)
    amax = np.abs(b).max(1)
    byte = np.clip(np.where(amax > 0, np.frexp(amax)[1] - 1 + 127 - 7, 1), 1, 254)
    codes = (b * np.exp2(127.0 - byte)[:, None, :]).reshape(n, m).astype(np.float32).astype(ml_dtypes.float8_e4m3fn).view(np.uint8)
    words = codes.reshape(n // 512, 128, 4, m).transpose(0, 1, 3, 2)
    return np.ascontiguousarray(words), np.ascontiguousarray(byte.astype(np.uint8).reshape(n // 512, 16, m))


R, N, M, J = 1024, 1024, 1024, 1024

EPS = 2.0


def setup_inputs():
    s, t = mx_kscale(N), mx_kscale(M)
    return {
        "c1": bf(np.random.standard_normal((R, N)) / np.sqrt(N) * s[None, :]),
        "plan": bf(np.random.standard_normal((N, M)) / s[:, None] * t[None, :]),
        "c2": bf(np.random.standard_normal((J, M)) / np.sqrt(M) / t[None, :]),
        "cost": bf(np.random.standard_normal((R, J))),
        "v": bf(0.5 * np.random.standard_normal(J)),
        "r": bf(np.random.uniform(0.5, 1.5, R)),
    }


def gromov_product(c1, plan, c2):
    y = mxq(c1, 1, "e4m3") @ mxq(plan, 0, "e4m3")
    return mxq(y, 1, "e4m3") @ mxq(c2, 1, "e4m3").T


def core(c1, plan, c2, cost, v, r):
    g = gromov_product(f64(c1), f64(plan), f64(c2))
    logits = f64(v)[None, :] + (2.0 * g - f64(cost)) / EPS
    e = np.exp(logits - logits.max(axis=1, keepdims=True))
    q = e / e.sum(axis=1, keepdims=True)
    columns = plan.shape[1]
    return columns * f64(r)[:, None] * q


def reference(c1, plan, c2, cost, v, r):
    R_out = core(c1, plan, c2, cost, v, r)
    words, scales = planes(R_out)
    return R_out, words, scales

@@ -1,0 +1,549 @@
+from contextlib import ExitStack
+
+import concourse.mybir as mybir
+from concourse.masks import make_identity
+
+F32 = mybir.dt.float32
+BF16 = mybir.dt.bfloat16
+U32 = mybir.dt.uint32
+I32 = mybir.dt.int32
+U8 = mybir.dt.uint8
+FP8X4 = mybir.dt.float8_e4m3fn_x4
+ALU = mybir.AluOpType
+ACT = mybir.ActivationFunctionType
+AX = mybir.AxisListType
+
+P = 128
+D = 1024
+FLOPS = 2 * 2 * D * D * D
+
+
+def tile_fusedgromovwassersteinsinkhornhalfstep_x1_kernel(tc, c1, plan, c2, cost, v, r, out, words_out, scales_out):
+    nc = tc.nc
+    c1v = c1.rearrange("(g p t) n -> g t p n", g=2, p=P, t=4)
+    planv = plan.rearrange("(q p j) m -> q p j m", q=2, p=P, j=4)
+    c2v = c2.rearrange("(c h p) m -> c p h m", c=4, h=2, p=P)
+    costv = cost.rearrange("(g p t) n -> g t p n", g=2, p=P, t=4)
+    outv = out.rearrange("(g p t) n -> g t p n", g=2, p=P, t=4)
+
+    with ExitStack() as ctx:
+        const = ctx.enter_context(tc.tile_pool(name="const", bufs=1))
+        raw = ctx.enter_context(tc.tile_pool(name="raw", bufs=1))
+        work = ctx.enter_context(tc.tile_pool(name="work", bufs=2))
+        codes = ctx.enter_context(tc.tile_pool(name="codes", bufs=1))
+        psum = ctx.enter_context(tc.psum_pool(name="psum", bufs=8))
+        ctx.enter_context(tc.manual_schedule())
+
+        dummy = const.tile([P, 1], F32, name="dummy")
+        nc.vector.memset(dummy[:], 0.0)
+        dummy2 = const.tile([P, 1], F32, name="dummy2")
+        nc.scalar.activation(out=dummy2[:], in_=dummy[:], func=ACT.Exp)
+        ident = const.tile([P, P], F32, name="ident")
+        make_identity(nc, ident[:])
+        twos = const.tile([P, P], BF16, name="twos")
+        nc.vector.memset(twos[:], 2.0)
+        vrow = const.tile([P, D], BF16, name="vrow")
+        nc.vector.memset(vrow[:], 0.0)
+
+        c1_raw = {}
+        plan_raw = {}
+        c2_raw = {}
+        cost_raw = {}
+
+        def load_c1(k):
+            c1_raw[k] = raw.tile([P, D], BF16, name="c1_raw%d" % k)
+            nc.sync.dma_start(out=c1_raw[k][:], in_=c1v[k // 4, k % 4, :, :])
+
+        def load_plan(mg, q):
+            plan_raw[mg, q] = raw.tile([P, 4, 512], BF16, name="plan_raw%d%d" % (mg, q))
+            nc.sync.dma_start(out=plan_raw[mg, q][:], in_=planv[q, :, :, 512 * mg : 512 * mg + 512])
+
+        def load_c2(c):
+            c2_raw[c] = raw.tile([P, 2, D], BF16, name="c2_raw%d" % c)
+            nc.sync.dma_start(out=c2_raw[c][:], in_=c2v[c, :, :, :])
+
+        def load_cost(k):
+            cost_raw[k] = raw.tile([P, D], BF16, name="cost_raw%d" % k)
+            nc.sync.dma_start(out=cost_raw[k][:], in_=costv[k // 4, k % 4, :, :])
+
+        r_sb = const.tile([P, 2, 4], BF16, name="r_sb")
+
+        def load_v():
+            nc.sync.dma_start(out=vrow[0:1, :], in_=v.rearrange("(o n) -> o n", o=1))
+
+        def load_r():
+            nc.sync.dma_start(out=r_sb[:], in_=r.rearrange("(g p t) -> p g t", g=2, p=P, t=4))
+
+        c1_codes = {}
+        c1_scales = {}
+        c1_grp = {}
+        plan_codes = {}
+        plan_scales = {}
+        plan_grp = {}
+        c2_codes = {}
+        c2_scales = {}
+        c2_grp = {}
+        y_codes = {}
+        y_scales = {}
+        y_grp = {}
+        y_bank = {}
+        tr_bank = {}
+        d2 = {}
+        o_t = {}
+        g_bank = {}
+        x_t = {}
+        e_t = {}
+        nmax_t = {}
+        total_t = {}
+        rec_t = {}
+        fac_t = {}
+        ob_t = {}
+        w_t = {}
+        s_t = {}
+        for jh in range(2):
+            for mg in range(2):
+                c2_codes[jh, mg] = codes.tile([P, 512], U32, name="c2_codes%d%d" % (jh, mg), align_bytes=64)
+                c2_scales[jh, mg] = codes.tile([P, 512], U8, name="c2_scales%d%d" % (jh, mg), align_bytes=64)
+
+        def quant(out_codes, out_scales, in_):
+            nc.vector.quantize_mx(out=out_codes.bitcast(FP8X4), scales=out_scales, in_=in_)
+
+        def copy_on(eng, out, in_):
+            if eng == "S":
+                nc.scalar.copy(out=out, in_=in_)
+            elif eng == "V":
+                nc.vector.tensor_copy(out=out, in_=in_)
+            else:
+                nc.gpsimd.tensor_scalar(out=out, in0=in_, scalar1=1.0, scalar2=0.0, op0=ALU.mult, op1=ALU.add)
+
+        def turn(bank, words):
+            for q in range(2):
+                for u in range(2):
+                    nc.tensor.transpose(bank[:, 2 * q + u, :], words[:, 256 * q + u : 256 * (q + 1) : 2], ident[:])
+
+        def a_tr(k):
+            tr_bank[k] = psum.tile([P, 4, P], F32, name="tr_bank", tag="bank")
+            turn(tr_bank[k], c1_raw[k][:].bitcast(F32))
+
+        def a_cp(k, eng):
+            c1_grp[k] = work.tile([P, 2, P, 4], BF16, name="c1_grp", tag="c1_grp", bufs=4, align_bytes=64)
+            copy_on(
+                eng,
+                c1_grp[k][:].rearrange("p q r t -> p (q r t)").bitcast(F32).rearrange("p (q r u) -> p q r u", q=2, u=2),
+                tr_bank[k][:].rearrange("p (q u) r -> p q r u", q=2),
+            )
+
+        def a_q(k):
+            c1_codes[k] = codes.tile([P, 2, P], U32, name="c1_codes%d" % k, align_bytes=64)
+            c1_scales[k] = codes.tile([P, 2, P], U8, name="c1_scales%d" % k, align_bytes=64)
+            quant(
+                c1_codes[k][:].rearrange("p q r -> p (q r)"),
+                c1_scales[k][:].rearrange("p q r -> p (q r)"),
+                c1_grp[k][:].rearrange("p q r t -> p (q r t)"),
+            )
+
+        def p_cp(mg, q, eng):
+            plan_grp[mg, q] = work.tile([P, 2048], BF16, name="plan_grp", tag="plan_grp", bufs=3, align_bytes=64)
+            copy_on(
+                eng,
+                plan_grp[mg, q][:].rearrange("p (t m j) -> p t m j", t=4, j=4),
+                plan_raw[mg, q][:].rearrange("p j (m t) -> p t m j", t=4),
+            )
+
+        def p_q(mg, q):
+            plan_codes[mg, q] = codes.tile([P, 512], U32, name="plan_codes%d%d" % (mg, q), align_bytes=64)
+            plan_scales[mg, q] = codes.tile([P, 512], U8, name="plan_scales%d%d" % (mg, q), align_bytes=64)
+            quant(plan_codes[mg, q][:], plan_scales[mg, q][:], plan_grp[mg, q][:])
+
+        def b_mm(k, mg):
+            y_bank[k, mg] = psum.tile([P, 4, P], F32, name="y_bank", tag="bank")
+            for t in range(4):
+                for q in range(2):
+                    nc.tensor.matmul_mx(
+                        out=y_bank[k, mg][:, t, :],
+                        lhsT=plan_codes[mg, q][:, P * t : P * t + P].bitcast(FP8X4),
+                        lhsT_scale=plan_scales[mg, q][:, P * t : P * t + P],
+                        rhs=c1_codes[k][:, q, :].bitcast(FP8X4),
+                        rhs_scale=c1_scales[k][:, q, :],
+                        start=(q == 0),
+                        stop=(q == 1),
+                    )
+
+        def b_cp(k, mg, eng):
+            if k not in y_grp:
+                y_grp[k] = work.tile([P, 2, P, 4], BF16, name="y_grp", tag="y_grp", bufs=3, align_bytes=64)
+            copy_on(eng, y_grp[k][:, mg, :, :], y_bank[k, mg][:].rearrange("p t n -> p n t"))
+
+        def b_q(k):
+            y_codes[k] = codes.tile([P, 2, P], U32, name="y_codes%d" % k, align_bytes=64)
+            y_scales[k] = codes.tile([P, 2, P], U8, name="y_scales%d" % k, align_bytes=64)
+            quant(
+                y_codes[k][:].rearrange("p q r -> p (q r)"),
+                y_scales[k][:].rearrange("p q r -> p (q r)"),
+                y_grp[k][:].rearrange("p q r t -> p (q r t)"),
+            )
+
+        def e_tr(c, h):
+            tr_bank["c2", c, h] = psum.tile([P, 4, P], F32, name="tr_bank2", tag="bank")
+            turn(tr_bank["c2", c, h], c2_raw[c][:, h, :].bitcast(F32))
+
+        def e_cp(c, h, eng):
+            if c not in c2_grp:
+                c2_grp[c] = work.tile([P, 2, 256, 4], BF16, name="c2_grp", tag="c2_grp", bufs=2, align_bytes=64)
+            words = c2_grp[c][:].rearrange("p q r t -> p (q r t)").bitcast(F32).rearrange("p (q r u) -> p q r u", q=2, u=2)
+            copy_on(eng, words[:, :, P * h : P * h + P, :], tr_bank["c2", c, h][:].rearrange("p (q u) r -> p q r u", q=2))
+
+        def e_q(c):
+            jh = c // 2
+            cols = slice(256 * (c % 2), 256 * (c % 2) + 256)
+            for mg in range(2):
+                quant(c2_codes[jh, mg][:, cols], c2_scales[jh, mg][:, cols], c2_grp[c][:, mg, :, :].rearrange("p r t -> p (r t)"))
+
+        v2 = const.tile([P, D], BF16, name="v2")
+
+        v_bank = {}
+
+        def v_mm():
+            for jh in range(2):
+                v_bank[jh] = psum.tile([P, 512], F32, name="v_bank", tag="bank")
+                nc.tensor.matmul(v_bank[jh][:], lhsT=twos[:], rhs=vrow[:, 512 * jh : 512 * jh + 512], start=True, stop=True)
+
+        def v_cp():
+            for jh in range(2):
+                nc.scalar.copy(out=v2[:, 512 * jh : 512 * jh + 512], in_=v_bank[jh][:])
+
+        def d_tt(k, jh):
+            d2[k, jh] = work.tile([P, 512], F32, name="d2", tag="d2", bufs=6)
+            cols = slice(512 * jh, 512 * jh + 512)
+            nc.gpsimd.tensor_tensor(out=d2[k, jh][:], in0=v2[:, cols], in1=cost_raw[k][:, cols], op=ALU.subtract)
+
+        def c_mm(k, jh):
+            g_bank[k, jh] = psum.tile([P, 512], F32, name="g_bank", tag="bank")
+            for mg in range(2):
+                nc.tensor.matmul_mx(
+                    out=g_bank[k, jh][:],
+                    lhsT=y_codes[k][:, mg, :].bitcast(FP8X4),
+                    lhsT_scale=y_scales[k][:, mg, :],
+                    rhs=c2_codes[jh, mg][:].bitcast(FP8X4),
+                    rhs_scale=c2_scales[jh, mg][:],
+                    start=(mg == 0),
+                    stop=(mg == 1),
+                )
+
+        def c_x(k, jh):
+            if k not in x_t:
+                x_t[k] = work.tile([P, D], F32, name="x", tag="x", bufs=3)
+            cols = slice(512 * jh, 512 * jh + 512)
+            nc.vector.scalar_tensor_tensor(
+                out=x_t[k][:, cols], in0=d2[k, jh][:], scalar=0.5, in1=g_bank[k, jh][:], op0=ALU.mult, op1=ALU.add
+            )
+
+        def c_max(k):
+            nmax_t[k] = work.tile([P, 1], F32, name="nmax", tag="nmax", bufs=3)
+            nc.vector.tensor_reduce(out=nmax_t[k][:], in_=x_t[k][:], axis=AX.X, op=ALU.max, negate=True)
+
+        def c_exp(k):
+            e_t[k] = work.tile([P, D], F32, name="e", tag="e", bufs=3)
+            total_t[k] = work.tile([P, 1], F32, name="total", tag="total", bufs=3)
+            nc.scalar.activation(
+                out=e_t[k][:], in_=x_t[k][:], func=ACT.Exp, bias=nmax_t[k][:], scale=1.0, accum_out=total_t[k][:]
+            )
+
+        def c_rec(k):
+            rec_t[k] = work.tile([P, 1], F32, name="rec", tag="rec", bufs=3)
+            nc.vector.reciprocal(rec_t[k][:], total_t[k][:])
+
+        def c_fac(k):
+            fac_t[k] = work.tile([P, 1], F32, name="fac", tag="fac", bufs=3)
+            nc.vector.tensor_scalar(
+                out=fac_t[k][:],
+                in0=rec_t[k][:],
+                scalar1=r_sb[:, k // 4, k % 4 : k % 4 + 1],
+                scalar2=float(D),
+                op0=ALU.mult,
+                op1=ALU.mult,
+            )
+
+        def c_sc(k, eng):
+            g, t = k // 4, k % 4
+            if g not in o_t:
+                o_t[g] = work.tile([P, 4, D], F32, name="o_t", tag="o_t", bufs=2)
+            if eng == "S":
+                nc.scalar.activation(out=o_t[g][:, t, :], in_=e_t[k][:], func=ACT.Copy, scale=fac_t[k][:])
+            else:
+                nc.vector.tensor_scalar(
+                    out=o_t[g][:, t, :], in0=e_t[k][:], scalar1=fac_t[k][:], scalar2=None, op0=ALU.mult
+                )
+
+        def c_store(k):
+            g, t = k // 4, k % 4
+            nc.sync.dma_start(out=outv[g, t, :, :], in_=o_t[g][:, t, :])
+
+        def f_cp(g, h, eng):
+            ob_t[g, h] = work.tile([P, 256, 4], BF16, name="ob", tag="ob", bufs=4, align_bytes=64)
+            cols = slice(256 * h, 256 * h + 256)
+            copy_on(eng, ob_t[g, h][:], o_t[g][:, :, cols].rearrange("p t n -> p n t"))
+
+        def f_q(g, h):
+            if g not in w_t:
+                w_t[g] = work.tile([P, D], U32, name="w", tag="w", bufs=2, align_bytes=64)
+                s_t[g] = work.tile([P, D], U8, name="s", tag="s", bufs=2, align_bytes=64)
+            cols = slice(256 * h, 256 * h + 256)
+            quant(w_t[g][:, cols], s_t[g][:, cols], ob_t[g, h][:].rearrange("p n t -> p (n t)"))
+
+        def f_store(g, h):
+            cols = slice(256 * h, 256 * h + 256)
+            nc.sync.dma_start(
+                out=words_out[g, :, cols, :].rearrange("p n t -> p (n t)").bitcast(I32),
+                in_=w_t[g][:, cols].bitcast(I32),
+            )
+
+        def f_s(g):
+            for a in range(4):
+                nc.sync.dma_start(
+                    out=scales_out[g, 4 * a : 4 * a + 4, :].bitcast(I32), in_=s_t[g][32 * a : 32 * a + 4, :].bitcast(I32)
+                )
+
+
+        load_plan(0, 0)
+        p_cp(0, 0, "V")
+        p_q(0, 0)
+        load_v()
+        v_mm()
+        v_cp()
+        load_c1(0)
+        a_tr(0)
+        a_cp(0, "S")
+        load_plan(0, 1)
+        p_cp(0, 1, "V")
+        load_c1(1)
+        a_tr(1)
+        load_plan(1, 0)
+        load_c1(2)
+        a_tr(2)
+        a_q(0)
+        load_cost(0)
+        d_tt(0, 1)
+        p_q(0, 1)
+        load_c1(4)
+        a_tr(4)
+        load_plan(1, 1)
+        a_cp(1, "S")
+        p_cp(1, 0, "S")
+        p_cp(1, 1, "S")
+        a_q(1)
+        a_cp(2, "V")
+        a_q(2)
+        b_mm(1, 0)
+        b_mm(0, 0)
+        b_cp(0, 0, "S")
+        a_cp(4, "V")
+        a_q(4)
+        b_mm(2, 0)
+        load_c2(0)
+        e_tr(0, 0)
+        p_q(1, 0)
+        load_cost(1)
+        load_c2(2)
+        e_tr(0, 1)
+        e_cp(0, 0, "V")
+        e_tr(2, 1)
+        d_tt(0, 0)
+        b_cp(2, 0, "S")
+        e_tr(2, 0)
+        load_cost(4)
+        d_tt(1, 1)
+        p_q(1, 1)
+        b_mm(1, 1)
+        e_cp(0, 1, "V")
+        e_q(0)
+        d_tt(4, 1)
+        b_cp(1, 0, "S")
+        e_cp(2, 1, "V")
+        b_mm(0, 1)
+        load_c2(3)
+        e_cp(2, 0, "S")
+        e_q(2)
+        b_mm(2, 1)
+        b_cp(2, 1, "S")
+        d_tt(1, 0)
+        load_c2(1)
+        e_tr(1, 1)
+        b_cp(1, 1, "V")
+        b_cp(0, 1, "S")
+        e_tr(3, 0)
+        e_cp(3, 0, "V")
+        b_q(2)
+        load_cost(3)
+        e_tr(1, 0)
+        e_cp(1, 1, "S")
+        d_tt(4, 0)
+        e_cp(1, 0, "S")
+        e_q(1)
+        load_c1(3)
+        load_cost(7)
+        a_tr(3)
+        a_cp(3, "S")
+        load_c1(7)
+        e_tr(3, 1)
+        a_tr(7)
+        e_cp(3, 1, "S")
+        load_c1(6)
+        a_tr(6)
+        a_cp(6, "S")
+        b_q(0)
+        c_mm(0, 0)
+        b_mm(4, 0)
+        b_q(1)
+        e_q(3)
+        c_mm(0, 1)
+        a_cp(7, "S")
+        a_q(3)
+        b_cp(4, 0, "S")
+        c_x(0, 0)
+        a_q(6)
+        a_q(7)
+        c_x(0, 1)
+        c_max(0)
+        load_c1(5)
+        b_mm(4, 1)
+        b_cp(4, 1, "S")
+        b_q(4)
+        a_tr(5)
+        a_cp(5, "S")
+        c_mm(1, 1)
+        c_x(1, 1)
+        c_exp(0)
+        c_mm(1, 0)
+        b_mm(6, 1)
+        b_cp(6, 1, "S")
+        c_x(1, 0)
+        load_cost(6)
+        a_q(5)
+        load_cost(2)
+        load_cost(5)
+        load_r()
+        b_mm(6, 0)
+        b_cp(6, 0, "S")
+        d_tt(2, 0)
+        d_tt(6, 0)
+        c_max(1)
+        c_rec(0)
+        b_q(6)
+        c_fac(0)
+        b_mm(3, 0)
+        b_cp(3, 0, "S")
+        c_mm(2, 0)
+        c_x(2, 0)
+        c_mm(4, 1)
+        c_x(4, 1)
+        d_tt(2, 1)
+        c_mm(2, 1)
+        c_exp(1)
+        c_rec(1)
+        c_sc(0, "S")
+        b_mm(3, 1)
+        b_cp(3, 1, "S")
+        c_mm(4, 0)
+        d_tt(3, 0)
+        b_mm(7, 1)
+        c_x(2, 1)
+        c_fac(1)
+        c_sc(1, "S")
+        b_mm(7, 0)
+        c_max(2)
+        c_x(4, 0)
+        b_cp(7, 0, "S")
+        b_q(3)
+        c_max(4)
+        d_tt(5, 0)
+        b_mm(5, 0)
+        c_store(0)
+        d_tt(3, 1)
+        c_mm(6, 0)
+        d_tt(6, 1)
+        b_cp(7, 1, "S")
+        b_q(7)
+        c_mm(3, 1)
+        c_x(3, 1)
+        c_x(6, 0)
+        b_mm(5, 1)
+        c_mm(6, 1)
+        c_exp(2)
+        c_rec(2)
+        c_mm(3, 0)
+        c_x(3, 0)
+        c_mm(7, 1)
+        c_x(6, 1)
+        c_fac(2)
+        b_cp(5, 0, "S")
+        b_cp(5, 1, "S")
+        c_max(3)
+        c_store(1)
+        b_q(5)
+        d_tt(5, 1)
+        c_mm(5, 0)
+        c_max(6)
+        c_exp(4)
+        d_tt(7, 1)
+        c_sc(2, "S")
+        c_x(5, 0)
+        c_exp(3)
+        d_tt(7, 0)
+        c_rec(3)
+        c_rec(4)
+        c_fac(3)
+        c_exp(6)
+        c_fac(4)
+        c_sc(4, "S")
+        c_sc(3, "V")
+        c_store(2)
+        c_rec(6)
+        f_cp(0, 1, "G")
+        f_cp(0, 3, "S")
+        c_mm(5, 1)
+        c_x(5, 1)
+        f_cp(0, 0, "G")
+        c_fac(6)
+        c_sc(6, "S")
+        c_mm(7, 0)
+        c_max(5)
+        c_exp(5)
+        c_x(7, 1)
+        c_x(7, 0)
+        c_max(7)
+        c_exp(7)
+        c_store(3)
+        f_q(0, 0)
+        c_rec(5)
+        c_store(4)
+        f_cp(0, 2, "G")
+        c_store(6)
+        f_q(0, 1)
+        c_fac(5)
+        c_sc(5, "S")
+        f_store(0, 1)
+        f_q(0, 2)
+        f_q(0, 3)
+        f_store(0, 3)
+        f_store(0, 2)
+        c_rec(7)
+        c_fac(7)
+        f_store(0, 0)
+        f_s(0)
+        c_sc(7, "V")
+        f_cp(1, 2, "V")
+        f_q(1, 2)
+        c_store(7)
+        f_cp(1, 3, "S")
+        c_store(5)
+        f_cp(1, 0, "V")
+        f_store(1, 2)
+        f_q(1, 3)
+        f_q(1, 0)
+        f_store(1, 3)
+        f_store(1, 0)
+        f_cp(1, 1, "S")
+        f_q(1, 1)
+        f_store(1, 1)
+        f_s(1)

@@ -21,9 +21,10 @@ FLOPS = 2 * 2 * D * D * D
 def tile_fusedgromovwassersteinsinkhornhalfstep_x1_kernel(tc, c1, plan, c2, cost, v, r, out, words_out, scales_out):
     nc = tc.nc
     c1v = c1.rearrange("(g p t) n -> g t p n", g=2, p=P, t=4)
+    c1w = c1.rearrange("(g p s u) n -> g s p u n", g=2, p=P, s=2, u=2)
     planv = plan.rearrange("(q p j) m -> q p j m", q=2, p=P, j=4)
-    c2v = c2.rearrange("(c h p) m -> c p h m", c=4, h=2, p=P)
-    costv = cost.rearrange("(g p t) n -> g t p n", g=2, p=P, t=4)
+    c2v = c2.rearrange("(c p h) m -> c p h m", c=4, p=P, h=2)
+    costv = cost.rearrange("(g p s u) n -> g s p u n", g=2, p=P, s=2, u=2)
     outv = out.rearrange("(g p t) n -> g t p n", g=2, p=P, t=4)
 
     with ExitStack() as ctx:
@@ -50,29 +51,44 @@ def tile_fusedgromovwassersteinsinkhornhalfstep_x1_kernel(tc, c1, plan, c2, cost
         c2_raw = {}
         cost_raw = {}
 
-        def load_c1(k):
-            c1_raw[k] = raw.tile([P, D], BF16, name="c1_raw%d" % k)
-            nc.sync.dma_start(out=c1_raw[k][:], in_=c1v[k // 4, k % 4, :, :])
+        def load_c1(i):
+            if i < 2:
+                c1_one = raw.tile([P, D], BF16, name="c1_one%d" % i)
+                nc.sync.dma_start(out=c1_one[:], in_=c1v[0, i, :, :])
+                c1_raw[i] = c1_one[:]
+            else:
+                k = 2 * i - 2
+                c1_two = raw.tile([P, 2, D], BF16, name="c1_two%d" % i)
+                nc.sync.dma_start(out=c1_two[:], in_=c1w[k // 4, (k % 4) // 2, :, :, :])
+                c1_raw[k] = c1_two[:, 0, :]
+                c1_raw[k + 1] = c1_two[:, 1, :]
 
-        def load_plan(mg, q):
-            plan_raw[mg, q] = raw.tile([P, 4, 512], BF16, name="plan_raw%d%d" % (mg, q))
-            nc.sync.dma_start(out=plan_raw[mg, q][:], in_=planv[q, :, :, 512 * mg : 512 * mg + 512])
+        def load_plan(q):
+            plan_raw[q] = raw.tile([P, 4, D], BF16, name="plan_raw%d" % q)
+            nc.sync.dma_start(out=plan_raw[q][:], in_=planv[q, :, :, :])
 
         def load_c2(c):
             c2_raw[c] = raw.tile([P, 2, D], BF16, name="c2_raw%d" % c)
             nc.sync.dma_start(out=c2_raw[c][:], in_=c2v[c, :, :, :])
 
-        def load_cost(k):
-            cost_raw[k] = raw.tile([P, D], BF16, name="cost_raw%d" % k)
-            nc.sync.dma_start(out=cost_raw[k][:], in_=costv[k // 4, k % 4, :, :])
+        def load_cost(i):
+            cost_two = raw.tile([P, 2, D], BF16, name="cost_two%d" % i)
+            nc.sync.dma_start(out=cost_two[:], in_=costv[i // 2, i % 2, :, :, :])
+            cost_raw[2 * i] = cost_two[:, 0, :]
+            cost_raw[2 * i + 1] = cost_two[:, 1, :]
 
         r_sb = const.tile([P, 2, 4], BF16, name="r_sb")
 
         def load_v():
             nc.sync.dma_start(out=vrow[0:1, :], in_=v.rearrange("(o n) -> o n", o=1))
 
+        r_all = const.tile([P, 2, 4], F32, name="r_all")
+
         def load_r():
             nc.sync.dma_start(out=r_sb[:], in_=r.rearrange("(g p t) -> p g t", g=2, p=P, t=4))
+
+        def r_times():
+            nc.vector.tensor_scalar(out=r_all[:], in0=r_sb[:], scalar1=float(D), scalar2=None, op0=ALU.mult)
 
         c1_codes = {}
         c1_scales = {}
@@ -123,7 +139,7 @@ def tile_fusedgromovwassersteinsinkhornhalfstep_x1_kernel(tc, c1, plan, c2, cost
 
         def a_tr(k):
             tr_bank[k] = psum.tile([P, 4, P], F32, name="tr_bank", tag="bank")
-            turn(tr_bank[k], c1_raw[k][:].bitcast(F32))
+            turn(tr_bank[k], c1_raw[k].bitcast(F32))
 
         def a_cp(k, eng):
             c1_grp[k] = work.tile([P, 2, P, 4], BF16, name="c1_grp", tag="c1_grp", bufs=4, align_bytes=64)
@@ -147,7 +163,7 @@ def tile_fusedgromovwassersteinsinkhornhalfstep_x1_kernel(tc, c1, plan, c2, cost
             copy_on(
                 eng,
                 plan_grp[mg, q][:].rearrange("p (t m j) -> p t m j", t=4, j=4),
-                plan_raw[mg, q][:].rearrange("p j (m t) -> p t m j", t=4),
+                plan_raw[q][:, :, 512 * mg : 512 * mg + 512].rearrange("p j (m t) -> p t m j", t=4),
             )
 
         def p_q(mg, q):
@@ -183,21 +199,26 @@ def tile_fusedgromovwassersteinsinkhornhalfstep_x1_kernel(tc, c1, plan, c2, cost
                 y_grp[k][:].rearrange("p q r t -> p (q r t)"),
             )
 
-        def e_tr(c, h):
-            tr_bank["c2", c, h] = psum.tile([P, 4, P], F32, name="tr_bank2", tag="bank")
-            turn(tr_bank["c2", c, h], c2_raw[c][:, h, :].bitcast(F32))
+        def e_tr(c, q):
+            tr_bank["c2", c, q] = psum.tile([P, 2, 2, P], F32, name="c2_bank", tag="bank")
+            for h in range(2):
+                words = c2_raw[c][:, h, :].bitcast(F32)
+                for u in range(2):
+                    nc.tensor.transpose(
+                        tr_bank["c2", c, q][:, h, u, :], words[:, 256 * q + u : 256 * (q + 1) : 2], ident[:]
+                    )
 
-        def e_cp(c, h, eng):
-            if c not in c2_grp:
-                c2_grp[c] = work.tile([P, 2, 256, 4], BF16, name="c2_grp", tag="c2_grp", bufs=2, align_bytes=64)
-            words = c2_grp[c][:].rearrange("p q r t -> p (q r t)").bitcast(F32).rearrange("p (q r u) -> p q r u", q=2, u=2)
-            copy_on(eng, words[:, :, P * h : P * h + P, :], tr_bank["c2", c, h][:].rearrange("p (q u) r -> p q r u", q=2))
+        def e_cp(c, q, eng):
+            c2_grp[c, q] = work.tile([P, 1024], BF16, name="c2_grp", tag="c2_grp", bufs=4, align_bytes=64)
+            copy_on(
+                eng,
+                c2_grp[c, q][:].bitcast(F32).rearrange("p (r h u) -> p r h u", h=2, u=2),
+                tr_bank["c2", c, q][:].rearrange("p h u r -> p r h u"),
+            )
 
-        def e_q(c):
-            jh = c // 2
+        def e_q(c, q):
             cols = slice(256 * (c % 2), 256 * (c % 2) + 256)
-            for mg in range(2):
-                quant(c2_codes[jh, mg][:, cols], c2_scales[jh, mg][:, cols], c2_grp[c][:, mg, :, :].rearrange("p r t -> p (r t)"))
+            quant(c2_codes[c // 2, q][:, cols], c2_scales[c // 2, q][:, cols], c2_grp[c, q][:])
 
         v2 = const.tile([P, D], BF16, name="v2")
 
@@ -208,14 +229,15 @@ def tile_fusedgromovwassersteinsinkhornhalfstep_x1_kernel(tc, c1, plan, c2, cost
                 v_bank[jh] = psum.tile([P, 512], F32, name="v_bank", tag="bank")
                 nc.tensor.matmul(v_bank[jh][:], lhsT=twos[:], rhs=vrow[:, 512 * jh : 512 * jh + 512], start=True, stop=True)
 
-        def v_cp():
+        def v_cp(eng):
             for jh in range(2):
-                nc.scalar.copy(out=v2[:, 512 * jh : 512 * jh + 512], in_=v_bank[jh][:])
+                copy_on(eng, v2[:, 512 * jh : 512 * jh + 512], v_bank[jh][:])
 
-        def d_tt(k, jh):
+        def d_tt(k, jh, eng):
             d2[k, jh] = work.tile([P, 512], F32, name="d2", tag="d2", bufs=6)
             cols = slice(512 * jh, 512 * jh + 512)
-            nc.gpsimd.tensor_tensor(out=d2[k, jh][:], in0=v2[:, cols], in1=cost_raw[k][:, cols], op=ALU.subtract)
+            engine = nc.gpsimd if eng == "G" else nc.vector
+            engine.tensor_tensor(out=d2[k, jh][:], in0=v2[:, cols], in1=cost_raw[k][:, cols], op=ALU.subtract)
 
         def c_mm(k, jh):
             g_bank[k, jh] = psum.tile([P, 512], F32, name="g_bank", tag="bank")
@@ -258,17 +280,25 @@ def tile_fusedgromovwassersteinsinkhornhalfstep_x1_kernel(tc, c1, plan, c2, cost
             nc.vector.tensor_scalar(
                 out=fac_t[k][:],
                 in0=rec_t[k][:],
-                scalar1=r_sb[:, k // 4, k % 4 : k % 4 + 1],
-                scalar2=float(D),
+                scalar1=r_all[:, k // 4, k % 4 : k % 4 + 1],
+                scalar2=None,
                 op0=ALU.mult,
-                op1=ALU.mult,
             )
 
         def c_sc(k, eng):
             g, t = k // 4, k % 4
             if g not in o_t:
                 o_t[g] = work.tile([P, 4, D], F32, name="o_t", tag="o_t", bufs=2)
-            if eng == "S":
+            if eng == "G":
+                nc.gpsimd.tensor_scalar(
+                    out=o_t[g][:, t, :],
+                    in0=e_t[k][:],
+                    scalar1=rec_t[k][:],
+                    scalar2=r_all[:, g, t : t + 1],
+                    op0=ALU.mult,
+                    op1=ALU.mult,
+                )
+            elif eng == "S":
                 nc.scalar.activation(out=o_t[g][:, t, :], in_=e_t[k][:], func=ACT.Copy, scale=fac_t[k][:])
             else:
                 nc.vector.tensor_scalar(
@@ -291,8 +321,7 @@ def tile_fusedgromovwassersteinsinkhornhalfstep_x1_kernel(tc, c1, plan, c2, cost
             cols = slice(256 * h, 256 * h + 256)
             quant(w_t[g][:, cols], s_t[g][:, cols], ob_t[g, h][:].rearrange("p n t -> p (n t)"))
 
-        def f_store(g, h):
-            cols = slice(256 * h, 256 * h + 256)
+        def f_store(g, cols):
             nc.sync.dma_start(
                 out=words_out[g, :, cols, :].rearrange("p n t -> p (n t)").bitcast(I32),
                 in_=w_t[g][:, cols].bitcast(I32),
@@ -305,245 +334,233 @@ def tile_fusedgromovwassersteinsinkhornhalfstep_x1_kernel(tc, c1, plan, c2, cost
                 )
 
 
-        load_plan(0, 0)
-        p_cp(0, 0, "V")
-        p_q(0, 0)
-        load_v()
-        v_mm()
-        v_cp()
         load_c1(0)
         a_tr(0)
         a_cp(0, "S")
-        load_plan(0, 1)
-        p_cp(0, 1, "V")
-        load_c1(1)
-        a_tr(1)
-        load_plan(1, 0)
+        a_q(0)
+        load_plan(1)
+        p_cp(1, 1, "V")
+        p_q(1, 1)
+        p_cp(0, 1, "S")
+        p_q(0, 1)
+        load_c2(0)
+        e_tr(0, 1)
+        e_tr(0, 0)
+        load_v()
+        v_mm()
+        e_cp(0, 1, "S")
+        e_q(0, 1)
+        load_plan(0)
+        p_cp(0, 0, "V")
+        p_q(0, 0)
         load_c1(2)
         a_tr(2)
-        a_q(0)
-        load_cost(0)
-        d_tt(0, 1)
-        p_q(0, 1)
-        load_c1(4)
-        a_tr(4)
-        load_plan(1, 1)
-        a_cp(1, "S")
-        p_cp(1, 0, "S")
-        p_cp(1, 1, "S")
-        a_q(1)
         a_cp(2, "V")
+        load_r()
+        a_tr(3)
+        load_c1(1)
+        e_cp(0, 0, "S")
+        load_cost(0)
+        e_q(0, 0)
         a_q(2)
-        b_mm(1, 0)
-        b_mm(0, 0)
-        b_cp(0, 0, "S")
-        a_cp(4, "V")
-        a_q(4)
-        b_mm(2, 0)
-        load_c2(0)
-        e_tr(0, 0)
+        a_tr(1)
+        p_cp(1, 0, "S")
         p_q(1, 0)
-        load_cost(1)
+        v_cp("S")
+        d_tt(0, 1, "G")
+        b_mm(0, 0)
+        d_tt(0, 0, "V")
         load_c2(2)
-        e_tr(0, 1)
-        e_cp(0, 0, "V")
-        e_tr(2, 1)
-        d_tt(0, 0)
-        b_cp(2, 0, "S")
-        e_tr(2, 0)
-        load_cost(4)
-        d_tt(1, 1)
-        p_q(1, 1)
-        b_mm(1, 1)
-        e_cp(0, 1, "V")
-        e_q(0)
-        d_tt(4, 1)
-        b_cp(1, 0, "S")
-        e_cp(2, 1, "V")
+        a_cp(1, "V")
+        b_mm(2, 0)
+        b_cp(2, 0, "V")
+        a_cp(3, "S")
+        a_q(3)
+        b_cp(0, 0, "S")
         b_mm(0, 1)
-        load_c2(3)
-        e_cp(2, 0, "S")
-        e_q(2)
+        b_cp(0, 1, "S")
+        b_q(0)
+        a_q(1)
         b_mm(2, 1)
         b_cp(2, 1, "S")
-        d_tt(1, 0)
-        load_c2(1)
-        e_tr(1, 1)
-        b_cp(1, 1, "V")
-        b_cp(0, 1, "S")
-        e_tr(3, 0)
-        e_cp(3, 0, "V")
         b_q(2)
-        load_cost(3)
-        e_tr(1, 0)
-        e_cp(1, 1, "S")
-        d_tt(4, 0)
-        e_cp(1, 0, "S")
-        e_q(1)
         load_c1(3)
-        load_cost(7)
-        a_tr(3)
-        a_cp(3, "S")
-        load_c1(7)
-        e_tr(3, 1)
-        a_tr(7)
-        e_cp(3, 1, "S")
-        load_c1(6)
-        a_tr(6)
-        a_cp(6, "S")
-        b_q(0)
-        c_mm(0, 0)
-        b_mm(4, 0)
-        b_q(1)
-        e_q(3)
-        c_mm(0, 1)
-        a_cp(7, "S")
-        a_q(3)
-        b_cp(4, 0, "S")
-        c_x(0, 0)
-        a_q(6)
-        a_q(7)
-        c_x(0, 1)
-        c_max(0)
-        load_c1(5)
-        b_mm(4, 1)
-        b_cp(4, 1, "S")
-        b_q(4)
+        e_tr(2, 0)
+        e_tr(2, 1)
+        d_tt(1, 1, "V")
+        e_cp(2, 0, "S")
+        e_q(2, 0)
+        e_cp(2, 1, "S")
+        load_cost(1)
+        a_tr(4)
+        a_cp(4, "S")
+        b_mm(3, 1)
+        d_tt(1, 0, "V")
+        d_tt(2, 0, "V")
+        a_q(4)
+        d_tt(2, 1, "V")
+        b_cp(3, 1, "S")
+        b_mm(3, 0)
+        load_c2(3)
+        b_cp(3, 0, "S")
+        b_q(3)
         a_tr(5)
         a_cp(5, "S")
+        e_tr(3, 1)
+        a_q(5)
+        e_cp(3, 1, "S")
+        e_q(3, 1)
+        load_c2(1)
+        e_tr(1, 1)
+        e_cp(1, 1, "S")
+        e_q(1, 1)
+        e_tr(1, 0)
+        e_cp(1, 0, "S")
+        load_c1(4)
+        a_tr(7)
+        e_q(1, 0)
+        d_tt(3, 0, "G")
+        e_q(2, 1)
+        a_cp(7, "S")
+        a_q(7)
+        e_tr(3, 0)
+        e_cp(3, 0, "S")
+        b_mm(1, 1)
+        load_cost(2)
+        b_cp(1, 1, "S")
+        c_mm(0, 0)
+        b_mm(1, 0)
+        b_cp(1, 0, "S")
+        e_q(3, 0)
+        c_mm(0, 1)
+        a_tr(6)
+        c_x(0, 0)
+        d_tt(3, 1, "G")
+        c_x(0, 1)
+        b_q(1)
+        c_max(0)
+        b_mm(7, 1)
+        c_mm(1, 0)
+        c_x(1, 0)
+        a_cp(6, "S")
+        c_exp(0)
+        d_tt(5, 0, "G")
         c_mm(1, 1)
         c_x(1, 1)
-        c_exp(0)
-        c_mm(1, 0)
-        b_mm(6, 1)
-        b_cp(6, 1, "S")
-        c_x(1, 0)
-        load_cost(6)
-        a_q(5)
-        load_cost(2)
-        load_cost(5)
-        load_r()
-        b_mm(6, 0)
-        b_cp(6, 0, "S")
-        d_tt(2, 0)
-        d_tt(6, 0)
-        c_max(1)
+        load_cost(3)
+        d_tt(6, 1, "G")
+        b_mm(5, 0)
+        a_q(6)
+        d_tt(4, 1, "G")
+        r_times()
         c_rec(0)
-        b_q(6)
-        c_fac(0)
-        b_mm(3, 0)
-        b_cp(3, 0, "S")
-        c_mm(2, 0)
-        c_x(2, 0)
-        c_mm(4, 1)
-        c_x(4, 1)
-        d_tt(2, 1)
+        d_tt(5, 1, "G")
+        b_mm(5, 1)
+        c_max(1)
+        b_cp(5, 0, "S")
+        b_cp(7, 1, "S")
         c_mm(2, 1)
+        c_fac(0)
+        b_cp(5, 1, "S")
+        c_sc(0, "S")
+        c_x(2, 1)
+        c_mm(2, 0)
+        c_mm(3, 1)
+        c_x(2, 0)
+        b_mm(4, 0)
+        c_mm(3, 0)
+        b_mm(6, 1)
+        d_tt(6, 0, "G")
+        b_mm(7, 0)
+        b_q(5)
+        b_cp(4, 0, "S")
+        c_max(2)
+        c_x(3, 1)
+        c_x(3, 0)
         c_exp(1)
         c_rec(1)
-        c_sc(0, "S")
-        b_mm(3, 1)
-        b_cp(3, 1, "S")
-        c_mm(4, 0)
-        d_tt(3, 0)
-        b_mm(7, 1)
-        c_x(2, 1)
-        c_fac(1)
-        c_sc(1, "S")
-        b_mm(7, 0)
-        c_max(2)
-        c_x(4, 0)
-        b_cp(7, 0, "S")
-        b_q(3)
-        c_max(4)
-        d_tt(5, 0)
-        b_mm(5, 0)
-        c_store(0)
-        d_tt(3, 1)
-        c_mm(6, 0)
-        d_tt(6, 1)
-        b_cp(7, 1, "S")
-        b_q(7)
-        c_mm(3, 1)
-        c_x(3, 1)
-        c_x(6, 0)
-        b_mm(5, 1)
-        c_mm(6, 1)
-        c_exp(2)
-        c_rec(2)
-        c_mm(3, 0)
-        c_x(3, 0)
-        c_mm(7, 1)
-        c_x(6, 1)
-        c_fac(2)
-        b_cp(5, 0, "S")
-        b_cp(5, 1, "S")
-        c_max(3)
-        c_store(1)
-        b_q(5)
-        d_tt(5, 1)
         c_mm(5, 0)
-        c_max(6)
-        c_exp(4)
-        d_tt(7, 1)
-        c_sc(2, "S")
         c_x(5, 0)
-        c_exp(3)
-        d_tt(7, 0)
-        c_rec(3)
-        c_rec(4)
-        c_fac(3)
-        c_exp(6)
-        c_fac(4)
-        c_sc(4, "S")
-        c_sc(3, "V")
-        c_store(2)
-        c_rec(6)
-        f_cp(0, 1, "G")
-        f_cp(0, 3, "S")
+        b_cp(6, 1, "S")
+        c_sc(1, "G")
         c_mm(5, 1)
+        c_store(0)
+        c_exp(2)
+        b_mm(4, 1)
+        b_cp(4, 1, "S")
         c_x(5, 1)
-        f_cp(0, 0, "G")
-        c_fac(6)
-        c_sc(6, "S")
-        c_mm(7, 0)
+        c_max(3)
+        b_mm(6, 0)
+        b_cp(6, 0, "S")
+        b_q(6)
+        c_mm(6, 1)
+        c_store(1)
+        d_tt(4, 0, "G")
+        c_rec(2)
+        c_mm(6, 0)
+        b_cp(7, 0, "S")
         c_max(5)
+        b_q(7)
+        c_exp(3)
+        c_mm(7, 1)
+        c_rec(3)
+        c_sc(2, "G")
+        c_store(2)
+        b_q(4)
+        c_mm(4, 1)
+        c_fac(3)
+        c_x(6, 1)
         c_exp(5)
-        c_x(7, 1)
-        c_x(7, 0)
-        c_max(7)
-        c_exp(7)
-        c_store(3)
-        f_q(0, 0)
         c_rec(5)
-        c_store(4)
-        f_cp(0, 2, "G")
-        c_store(6)
-        f_q(0, 1)
+        c_x(6, 0)
         c_fac(5)
+        c_sc(3, "S")
+        c_store(3)
+        c_max(6)
+        d_tt(7, 1, "G")
+        c_x(7, 1)
+        d_tt(7, 0, "G")
+        c_mm(4, 0)
+        c_x(4, 1)
         c_sc(5, "S")
-        f_store(0, 1)
+        c_store(5)
+        c_x(4, 0)
+        c_exp(6)
+        f_cp(0, 1, "S")
+        c_rec(6)
+        f_cp(0, 3, "S")
+        f_cp(0, 2, "G")
+        c_sc(6, "G")
+        c_store(6)
+        c_mm(7, 0)
+        c_x(7, 0)
+        c_max(4)
+        f_cp(0, 0, "G")
+        c_max(7)
         f_q(0, 2)
+        c_exp(4)
+        c_rec(4)
+        f_q(0, 1)
+        c_fac(4)
         f_q(0, 3)
-        f_store(0, 3)
-        f_store(0, 2)
-        c_rec(7)
-        c_fac(7)
-        f_store(0, 0)
+        f_q(0, 0)
+        f_store(0, slice(0, D))
         f_s(0)
+        c_exp(7)
+        c_rec(7)
+        c_sc(4, "S")
+        c_store(4)
+        c_fac(7)
         c_sc(7, "V")
+        f_cp(1, 3, "S")
+        f_cp(1, 1, "V")
         f_cp(1, 2, "V")
+        f_q(1, 3)
         f_q(1, 2)
         c_store(7)
-        f_cp(1, 3, "S")
-        c_store(5)
-        f_cp(1, 0, "V")
-        f_store(1, 2)
-        f_q(1, 3)
-        f_q(1, 0)
-        f_store(1, 3)
-        f_store(1, 0)
-        f_cp(1, 1, "S")
         f_q(1, 1)
-        f_store(1, 1)
+        f_store(1, slice(512, 1024))
+        f_cp(1, 0, "S")
+        f_q(1, 0)
+        f_store(1, slice(0, 512))
         f_s(1)

@@ -63,9 +63,16 @@ def tile_fusedgromovwassersteinsinkhornhalfstep_x1_kernel(tc, c1, plan, c2, cost
                 c1_raw[k] = c1_two[:, 0, :]
                 c1_raw[k + 1] = c1_two[:, 1, :]
 
-        def load_plan(q):
-            plan_raw[q] = raw.tile([P, 4, D], BF16, name="plan_raw%d" % q)
-            nc.sync.dma_start(out=plan_raw[q][:], in_=planv[q, :, :, :])
+        def load_plan(q, mg):
+            if mg is None:
+                whole = raw.tile([P, 4, D], BF16, name="plan_whole%d" % q)
+                nc.sync.dma_start(out=whole[:], in_=planv[q, :, :, :])
+                for half in range(2):
+                    plan_raw[half, q] = whole[:, :, 512 * half : 512 * half + 512]
+            else:
+                part = raw.tile([P, 4, 512], BF16, name="plan_part%d%d" % (mg, q))
+                nc.sync.dma_start(out=part[:], in_=planv[q, :, :, 512 * mg : 512 * mg + 512])
+                plan_raw[mg, q] = part[:]
 
         def load_c2(c):
             c2_raw[c] = raw.tile([P, 2, D], BF16, name="c2_raw%d" % c)
@@ -162,8 +169,8 @@ def tile_fusedgromovwassersteinsinkhornhalfstep_x1_kernel(tc, c1, plan, c2, cost
             plan_grp[mg, q] = work.tile([P, 2048], BF16, name="plan_grp", tag="plan_grp", bufs=3, align_bytes=64)
             copy_on(
                 eng,
-                plan_grp[mg, q][:].rearrange("p (t m j) -> p t m j", t=4, j=4),
-                plan_raw[q][:, :, 512 * mg : 512 * mg + 512].rearrange("p j (m t) -> p t m j", t=4),
+                plan_grp[mg, q][:].rearrange("p (t m j) -> p m j t", t=4, j=4),
+                plan_raw[mg, q].rearrange("p j (m t) -> p m j t", t=4),
             )
 
         def p_q(mg, q):
@@ -302,24 +309,45 @@ def tile_fusedgromovwassersteinsinkhornhalfstep_x1_kernel(tc, c1, plan, c2, cost
                 nc.scalar.activation(out=o_t[g][:, t, :], in_=e_t[k][:], func=ACT.Copy, scale=fac_t[k][:])
             else:
                 nc.vector.tensor_scalar(
-                    out=o_t[g][:, t, :], in0=e_t[k][:], scalar1=fac_t[k][:], scalar2=None, op0=ALU.mult
+                    out=o_t[g][:, t, :],
+                    in0=e_t[k][:],
+                    scalar1=rec_t[k][:],
+                    scalar2=r_all[:, g, t : t + 1],
+                    op0=ALU.mult,
+                    op1=ALU.mult,
                 )
+
+        def c_sc_half(k, h):
+            g, t = k // 4, k % 4
+            cols = slice(512 * h, 512 * h + 512)
+            nc.vector.tensor_scalar(
+                out=o_t[g][:, t, cols],
+                in0=e_t[k][:, cols],
+                scalar1=rec_t[k][:],
+                scalar2=r_all[:, g, t : t + 1],
+                op0=ALU.mult,
+                op1=ALU.mult,
+            )
 
         def c_store(k):
             g, t = k // 4, k % 4
             nc.sync.dma_start(out=outv[g, t, :, :], in_=o_t[g][:, t, :])
 
-        def f_cp(g, h, eng):
-            ob_t[g, h] = work.tile([P, 256, 4], BF16, name="ob", tag="ob", bufs=4, align_bytes=64)
-            cols = slice(256 * h, 256 * h + 256)
-            copy_on(eng, ob_t[g, h][:], o_t[g][:, :, cols].rearrange("p t n -> p n t"))
+        def f_cp(g, lo, hi, eng):
+            if g not in ob_t:
+                ob_t[g] = work.tile([P, D, 4], BF16, name="ob", tag="ob", bufs=2, align_bytes=64)
+            copy_on(
+                eng,
+                ob_t[g][:, lo:hi, :].rearrange("p (n i) t -> p n t i", i=4),
+                o_t[g][:, :, lo:hi].rearrange("p t (n i) -> p n t i", i=4),
+            )
 
         def f_q(g, h):
             if g not in w_t:
                 w_t[g] = work.tile([P, D], U32, name="w", tag="w", bufs=2, align_bytes=64)
                 s_t[g] = work.tile([P, D], U8, name="s", tag="s", bufs=2, align_bytes=64)
-            cols = slice(256 * h, 256 * h + 256)
-            quant(w_t[g][:, cols], s_t[g][:, cols], ob_t[g, h][:].rearrange("p n t -> p (n t)"))
+            cols = slice(512 * h, 512 * h + 512)
+            quant(w_t[g][:, cols], s_t[g][:, cols], ob_t[g][:, cols, :].rearrange("p n t -> p (n t)"))
 
         def f_store(g, cols):
             nc.sync.dma_start(
@@ -336,231 +364,228 @@ def tile_fusedgromovwassersteinsinkhornhalfstep_x1_kernel(tc, c1, plan, c2, cost
 
         load_c1(0)
         a_tr(0)
-        a_cp(0, "S")
+        load_c2(0)
+        load_plan(1, None)
+        a_cp(0, "V")
+        e_tr(0, 0)
+        e_tr(0, 1)
+        load_c1(1)
+        load_c1(2)
+        a_tr(1)
+        e_cp(0, 0, "S")
         a_q(0)
-        load_plan(1)
+        e_q(0, 0)
+        e_cp(0, 1, "V")
+        p_cp(0, 1, "S")
+        a_cp(1, "S")
+        a_tr(2)
+        a_cp(2, "S")
         p_cp(1, 1, "V")
         p_q(1, 1)
-        p_cp(0, 1, "S")
+        a_tr(3)
+        a_cp(3, "S")
         p_q(0, 1)
-        load_c2(0)
-        e_tr(0, 1)
-        e_tr(0, 0)
         load_v()
         v_mm()
-        e_cp(0, 1, "S")
-        e_q(0, 1)
-        load_plan(0)
-        p_cp(0, 0, "V")
-        p_q(0, 0)
-        load_c1(2)
-        a_tr(2)
-        a_cp(2, "V")
-        load_r()
-        a_tr(3)
-        load_c1(1)
-        e_cp(0, 0, "S")
-        load_cost(0)
-        e_q(0, 0)
-        a_q(2)
-        a_tr(1)
-        p_cp(1, 0, "S")
-        p_q(1, 0)
+        load_plan(0, 0)
         v_cp("S")
-        d_tt(0, 1, "G")
-        b_mm(0, 0)
-        d_tt(0, 0, "V")
-        load_c2(2)
-        a_cp(1, "V")
-        b_mm(2, 0)
-        b_cp(2, 0, "V")
-        a_cp(3, "S")
-        a_q(3)
-        b_cp(0, 0, "S")
-        b_mm(0, 1)
-        b_cp(0, 1, "S")
-        b_q(0)
         a_q(1)
-        b_mm(2, 1)
-        b_cp(2, 1, "S")
-        b_q(2)
+        p_cp(0, 0, "V")
+        load_c2(3)
+        e_tr(3, 1)
+        e_cp(3, 1, "S")
+        e_tr(3, 0)
+        a_q(3)
+        load_plan(0, 1)
         load_c1(3)
-        e_tr(2, 0)
+        p_q(0, 0)
+        b_mm(0, 0)
+        a_q(2)
+        e_cp(3, 0, "S")
+        load_c2(2)
+        e_q(0, 1)
+        p_cp(1, 0, "V")
+        b_mm(3, 0)
+        a_tr(5)
+        e_q(3, 1)
+        a_tr(4)
+        b_cp(3, 0, "S")
         e_tr(2, 1)
-        d_tt(1, 1, "V")
+        load_c2(1)
+        a_cp(5, "S")
+        p_q(1, 0)
+        a_cp(4, "S")
+        e_q(3, 0)
+        load_cost(1)
+        e_cp(2, 1, "S")
+        b_mm(3, 1)
+        b_cp(0, 0, "V")
+        a_q(5)
+        a_q(4)
+        e_tr(2, 0)
+        e_q(2, 1)
+        load_r()
+        d_tt(3, 1, "V")
+        b_cp(3, 1, "S")
+        b_q(3)
         e_cp(2, 0, "S")
         e_q(2, 0)
-        e_cp(2, 1, "S")
-        load_cost(1)
-        a_tr(4)
-        a_cp(4, "S")
-        b_mm(3, 1)
-        d_tt(1, 0, "V")
-        d_tt(2, 0, "V")
-        a_q(4)
-        d_tt(2, 1, "V")
-        b_cp(3, 1, "S")
-        b_mm(3, 0)
-        load_c2(3)
-        b_cp(3, 0, "S")
-        b_q(3)
-        a_tr(5)
-        a_cp(5, "S")
-        e_tr(3, 1)
-        a_q(5)
-        e_cp(3, 1, "S")
-        e_q(3, 1)
-        load_c2(1)
+        d_tt(3, 0, "V")
         e_tr(1, 1)
         e_cp(1, 1, "S")
         e_q(1, 1)
         e_tr(1, 0)
         e_cp(1, 0, "S")
-        load_c1(4)
-        a_tr(7)
         e_q(1, 0)
-        d_tt(3, 0, "G")
-        e_q(2, 1)
-        a_cp(7, "S")
-        a_q(7)
-        e_tr(3, 0)
-        e_cp(3, 0, "S")
-        b_mm(1, 1)
-        load_cost(2)
-        b_cp(1, 1, "S")
-        c_mm(0, 0)
-        b_mm(1, 0)
-        b_cp(1, 0, "S")
-        e_q(3, 0)
-        c_mm(0, 1)
-        a_tr(6)
-        c_x(0, 0)
-        d_tt(3, 1, "G")
-        c_x(0, 1)
-        b_q(1)
-        c_max(0)
-        b_mm(7, 1)
-        c_mm(1, 0)
-        c_x(1, 0)
-        a_cp(6, "S")
-        c_exp(0)
-        d_tt(5, 0, "G")
-        c_mm(1, 1)
-        c_x(1, 1)
-        load_cost(3)
-        d_tt(6, 1, "G")
-        b_mm(5, 0)
-        a_q(6)
-        d_tt(4, 1, "G")
-        r_times()
-        c_rec(0)
-        d_tt(5, 1, "G")
-        b_mm(5, 1)
-        c_max(1)
-        b_cp(5, 0, "S")
-        b_cp(7, 1, "S")
-        c_mm(2, 1)
-        c_fac(0)
-        b_cp(5, 1, "S")
-        c_sc(0, "S")
-        c_x(2, 1)
-        c_mm(2, 0)
+        b_mm(0, 1)
+        b_cp(0, 1, "S")
         c_mm(3, 1)
-        c_x(2, 0)
-        b_mm(4, 0)
-        c_mm(3, 0)
-        b_mm(6, 1)
-        d_tt(6, 0, "G")
-        b_mm(7, 0)
-        b_q(5)
-        b_cp(4, 0, "S")
-        c_max(2)
         c_x(3, 1)
+        b_mm(1, 0)
+        c_mm(3, 0)
+        b_cp(1, 0, "S")
+        b_mm(2, 1)
+        b_cp(2, 1, "S")
+        b_mm(2, 0)
+        b_cp(2, 0, "S")
+        load_c1(4)
+        b_q(0)
+        load_cost(0)
         c_x(3, 0)
-        c_exp(1)
-        c_rec(1)
-        c_mm(5, 0)
-        c_x(5, 0)
-        b_cp(6, 1, "S")
-        c_sc(1, "G")
-        c_mm(5, 1)
-        c_store(0)
-        c_exp(2)
-        b_mm(4, 1)
-        b_cp(4, 1, "S")
-        c_x(5, 1)
         c_max(3)
+        c_mm(0, 1)
+        c_mm(0, 0)
+        c_exp(3)
+        b_mm(1, 1)
+        b_cp(1, 1, "S")
+        a_tr(6)
+        a_cp(6, "S")
+        a_tr(7)
+        d_tt(0, 1, "G")
+        c_x(0, 1)
+        d_tt(0, 0, "G")
+        d_tt(2, 1, "G")
+        b_q(2)
+        c_mm(2, 0)
+        c_x(0, 0)
+        r_times()
+        c_rec(3)
+        c_fac(3)
+        c_max(0)
+        b_mm(5, 1)
+        b_q(1)
+        a_cp(7, "S")
+        load_cost(2)
+        a_q(7)
+        c_sc(3, "S")
+        d_tt(2, 0, "G")
+        b_mm(5, 0)
+        d_tt(1, 0, "G")
+        a_q(6)
+        c_x(2, 0)
+        b_cp(5, 1, "S")
+        c_exp(0)
+        c_mm(2, 1)
+        c_x(2, 1)
+        c_mm(1, 0)
+        c_max(2)
+        c_x(1, 0)
+        c_mm(1, 1)
+        b_cp(5, 0, "S")
+        load_cost(3)
+        b_q(5)
         b_mm(6, 0)
         b_cp(6, 0, "S")
+        d_tt(1, 1, "G")
+        b_mm(4, 0)
+        c_x(1, 1)
+        c_rec(0)
+        b_cp(4, 0, "S")
+        b_mm(6, 1)
+        b_cp(6, 1, "S")
+        b_mm(4, 1)
+        c_exp(2)
+        b_cp(4, 1, "S")
+        c_mm(5, 0)
+        c_max(1)
+        c_exp(1)
+        d_tt(5, 0, "G")
+        c_x(5, 0)
         b_q(6)
-        c_mm(6, 1)
-        c_store(1)
-        d_tt(4, 0, "G")
-        c_rec(2)
-        c_mm(6, 0)
+        c_fac(0)
+        b_mm(7, 0)
         b_cp(7, 0, "S")
+        c_rec(2)
+        d_tt(5, 1, "G")
+        c_mm(5, 1)
+        c_x(5, 1)
+        d_tt(6, 0, "G")
+        b_mm(7, 1)
+        c_rec(1)
+        c_store(3)
+        c_sc(0, "S")
+        c_store(0)
         c_max(5)
-        b_q(7)
-        c_exp(3)
-        c_mm(7, 1)
-        c_rec(3)
+        c_fac(1)
+        c_sc(1, "S")
+        c_mm(6, 0)
+        c_x(6, 0)
+        c_store(1)
+        c_exp(5)
+        c_mm(6, 1)
+        d_tt(6, 1, "G")
+        c_x(6, 1)
         c_sc(2, "G")
-        c_store(2)
+        f_cp(0, 768, 1024, "S")
         b_q(4)
         c_mm(4, 1)
-        c_fac(3)
-        c_x(6, 1)
-        c_exp(5)
-        c_rec(5)
-        c_x(6, 0)
-        c_fac(5)
-        c_sc(3, "S")
-        c_store(3)
+        d_tt(4, 1, "G")
+        d_tt(4, 0, "G")
+        b_cp(7, 1, "V")
+        c_store(2)
         c_max(6)
-        d_tt(7, 1, "G")
-        c_x(7, 1)
-        d_tt(7, 0, "G")
-        c_mm(4, 0)
-        c_x(4, 1)
-        c_sc(5, "S")
-        c_store(5)
-        c_x(4, 0)
         c_exp(6)
-        f_cp(0, 1, "S")
-        c_rec(6)
-        f_cp(0, 3, "S")
-        f_cp(0, 2, "G")
-        c_sc(6, "G")
-        c_store(6)
+        c_x(4, 1)
+        b_q(7)
+        c_mm(4, 0)
+        c_x(4, 0)
+        c_rec(5)
+        d_tt(7, 1, "G")
+        f_cp(0, 512, 768, "S")
+        f_cp(0, 0, 256, "S")
+        c_max(4)
+        c_mm(7, 1)
+        d_tt(7, 0, "G")
+        c_x(7, 1)
         c_mm(7, 0)
         c_x(7, 0)
-        c_max(4)
-        f_cp(0, 0, "G")
-        c_max(7)
-        f_q(0, 2)
+        c_rec(6)
         c_exp(4)
+        c_sc(5, "G")
+        c_max(7)
+        c_exp(7)
+        c_sc(6, "G")
         c_rec(4)
         f_q(0, 1)
-        c_fac(4)
-        f_q(0, 3)
-        f_q(0, 0)
-        f_store(0, slice(0, D))
-        f_s(0)
-        c_exp(7)
+        c_store(5)
+        c_store(6)
+        f_cp(0, 256, 512, "S")
+        c_sc(4, "V")
+        f_store(0, slice(512, 1024))
         c_rec(7)
-        c_sc(4, "S")
+        c_sc_half(7, 0)
+        c_sc_half(7, 1)
+        f_cp(1, 256, 512, "V")
         c_store(4)
-        c_fac(7)
-        c_sc(7, "V")
-        f_cp(1, 3, "S")
-        f_cp(1, 1, "V")
-        f_cp(1, 2, "V")
-        f_q(1, 3)
-        f_q(1, 2)
         c_store(7)
+        f_cp(1, 512, 640, "S")
+        f_cp(1, 0, 256, "V")
+        f_q(0, 0)
+        f_store(0, slice(0, 512))
+        f_s(0)
+        f_q(1, 0)
+        f_cp(1, 640, 1024, "S")
+        f_store(1, slice(0, 512))
         f_q(1, 1)
         f_store(1, slice(512, 1024))
-        f_cp(1, 0, "S")
-        f_q(1, 0)
-        f_store(1, slice(0, 512))
         f_s(1)

@@ -65,7 +65,7 @@ def tile_fusedgromovwassersteinsinkhornhalfstep_x1_kernel(tc, c1, plan, c2, cost
 
         def load_plan(q, mg):
             if mg is None:
-                whole = raw.tile([P, 4, D], BF16, name="plan_whole%d" % q)
+                whole = raw.tile([P, 4, D], BF16, name="plan_whole%d" % q, tag="plan_ob", bufs=2, align_bytes=64)
                 nc.sync.dma_start(out=whole[:], in_=planv[q, :, :, :])
                 for half in range(2):
                     plan_raw[half, q] = whole[:, :, 512 * half : 512 * half + 512]
@@ -231,17 +231,15 @@ def tile_fusedgromovwassersteinsinkhornhalfstep_x1_kernel(tc, c1, plan, c2, cost
 
         v_bank = {}
 
-        def v_mm():
-            for jh in range(2):
-                v_bank[jh] = psum.tile([P, 512], F32, name="v_bank", tag="bank")
-                nc.tensor.matmul(v_bank[jh][:], lhsT=twos[:], rhs=vrow[:, 512 * jh : 512 * jh + 512], start=True, stop=True)
+        def v_mm(jh):
+            v_bank[jh] = psum.tile([P, 512], F32, name="v_bank", tag="bank")
+            nc.tensor.matmul(v_bank[jh][:], lhsT=twos[:], rhs=vrow[:, 512 * jh : 512 * jh + 512], start=True, stop=True)
 
-        def v_cp(eng):
-            for jh in range(2):
-                copy_on(eng, v2[:, 512 * jh : 512 * jh + 512], v_bank[jh][:])
+        def v_cp(jh, eng):
+            copy_on(eng, v2[:, 512 * jh : 512 * jh + 512], v_bank[jh][:])
 
         def d_tt(k, jh, eng):
-            d2[k, jh] = work.tile([P, 512], F32, name="d2", tag="d2", bufs=6)
+            d2[k, jh] = work.tile([P, 512], F32, name="d2", tag="d2_%d" % jh, bufs=1)
             cols = slice(512 * jh, 512 * jh + 512)
             engine = nc.gpsimd if eng == "G" else nc.vector
             engine.tensor_tensor(out=d2[k, jh][:], in0=v2[:, cols], in1=cost_raw[k][:, cols], op=ALU.subtract)
@@ -335,12 +333,15 @@ def tile_fusedgromovwassersteinsinkhornhalfstep_x1_kernel(tc, c1, plan, c2, cost
 
         def f_cp(g, lo, hi, eng):
             if g not in ob_t:
-                ob_t[g] = work.tile([P, D, 4], BF16, name="ob", tag="ob", bufs=2, align_bytes=64)
-            copy_on(
-                eng,
-                ob_t[g][:, lo:hi, :].rearrange("p (n i) t -> p n t i", i=4),
-                o_t[g][:, :, lo:hi].rearrange("p t (n i) -> p n t i", i=4),
-            )
+                ob_t[g] = raw.tile([P, D, 4], BF16, name="ob", tag="plan_ob", bufs=2, align_bytes=64)
+            if eng == "G":
+                copy_on(eng, ob_t[g][:, lo:hi, :], o_t[g][:, :, lo:hi].rearrange("p t n -> p n t"))
+            else:
+                copy_on(
+                    eng,
+                    ob_t[g][:, lo:hi, :].rearrange("p (n i) t -> p n t i", i=4),
+                    o_t[g][:, :, lo:hi].rearrange("p t (n i) -> p n t i", i=4),
+                )
 
         def f_q(g, h):
             if g not in w_t:
@@ -386,9 +387,11 @@ def tile_fusedgromovwassersteinsinkhornhalfstep_x1_kernel(tc, c1, plan, c2, cost
         a_cp(3, "S")
         p_q(0, 1)
         load_v()
-        v_mm()
+        v_mm(0)
+        v_mm(1)
         load_plan(0, 0)
-        v_cp("S")
+        v_cp(0, "S")
+        v_cp(1, "S")
         a_q(1)
         p_cp(0, 0, "V")
         load_c2(3)

from contextlib import ExitStack

import concourse.mybir as mybir
from concourse.masks import make_identity

F32 = mybir.dt.float32
BF16 = mybir.dt.bfloat16
U32 = mybir.dt.uint32
I32 = mybir.dt.int32
U8 = mybir.dt.uint8
FP8X4 = mybir.dt.float8_e4m3fn_x4
ALU = mybir.AluOpType
ACT = mybir.ActivationFunctionType
AX = mybir.AxisListType

P = 128
D = 1024
FLOPS = 2 * 2 * D * D * D


def tile_fusedgromovwassersteinsinkhornhalfstep_x1_kernel(tc, c1, plan, c2, cost, v, r, out, words_out, scales_out):
    nc = tc.nc
    c1v = c1.rearrange("(g p t) n -> g t p n", g=2, p=P, t=4)
    c1w = c1.rearrange("(g p s u) n -> g s p u n", g=2, p=P, s=2, u=2)
    planv = plan.rearrange("(q p j) m -> q p j m", q=2, p=P, j=4)
    c2v = c2.rearrange("(c p h) m -> c p h m", c=4, p=P, h=2)
    costv = cost.rearrange("(g p s u) n -> g s p u n", g=2, p=P, s=2, u=2)
    outv = out.rearrange("(g p t) n -> g t p n", g=2, p=P, t=4)

    with ExitStack() as ctx:
        const = ctx.enter_context(tc.tile_pool(name="const", bufs=1))
        raw = ctx.enter_context(tc.tile_pool(name="raw", bufs=1))
        work = ctx.enter_context(tc.tile_pool(name="work", bufs=2))
        codes = ctx.enter_context(tc.tile_pool(name="codes", bufs=1))
        psum = ctx.enter_context(tc.psum_pool(name="psum", bufs=8))
        ctx.enter_context(tc.manual_schedule())

        dummy = const.tile([P, 1], F32, name="dummy")
        nc.vector.memset(dummy[:], 0.0)
        dummy2 = const.tile([P, 1], F32, name="dummy2")
        nc.scalar.activation(out=dummy2[:], in_=dummy[:], func=ACT.Exp)
        ident = const.tile([P, P], F32, name="ident")
        make_identity(nc, ident[:])
        twos = const.tile([P, P], BF16, name="twos")
        nc.vector.memset(twos[:], 2.0)
        vrow = const.tile([P, D], BF16, name="vrow")
        nc.vector.memset(vrow[:], 0.0)

        c1_raw = {}
        plan_raw = {}
        c2_raw = {}
        cost_raw = {}

        def load_c1(i):
            if i < 2:
                c1_one = raw.tile([P, D], BF16, name="c1_one%d" % i)
                nc.sync.dma_start(out=c1_one[:], in_=c1v[0, i, :, :])
                c1_raw[i] = c1_one[:]
            else:
                k = 2 * i - 2
                c1_two = raw.tile([P, 2, D], BF16, name="c1_two%d" % i)
                nc.sync.dma_start(out=c1_two[:], in_=c1w[k // 4, (k % 4) // 2, :, :, :])
                c1_raw[k] = c1_two[:, 0, :]
                c1_raw[k + 1] = c1_two[:, 1, :]

        def load_plan(q, mg):
            if mg is None:
                whole = raw.tile([P, 4, D], BF16, name="plan_whole%d" % q, tag="plan_ob", bufs=2, align_bytes=64)
                nc.sync.dma_start(out=whole[:], in_=planv[q, :, :, :])
                for half in range(2):
                    plan_raw[half, q] = whole[:, :, 512 * half : 512 * half + 512]
            else:
                part = raw.tile([P, 4, 512], BF16, name="plan_part%d%d" % (mg, q))
                nc.sync.dma_start(out=part[:], in_=planv[q, :, :, 512 * mg : 512 * mg + 512])
                plan_raw[mg, q] = part[:]

        def load_c2(c):
            c2_raw[c] = raw.tile([P, 2, D], BF16, name="c2_raw%d" % c)
            nc.sync.dma_start(out=c2_raw[c][:], in_=c2v[c, :, :, :])

        def load_cost(i):
            cost_two = raw.tile([P, 2, D], BF16, name="cost_two%d" % i)
            nc.sync.dma_start(out=cost_two[:], in_=costv[i // 2, i % 2, :, :, :])
            cost_raw[2 * i] = cost_two[:, 0, :]
            cost_raw[2 * i + 1] = cost_two[:, 1, :]

        r_sb = const.tile([P, 2, 4], BF16, name="r_sb")

        def load_v():
            nc.sync.dma_start(out=vrow[0:1, :], in_=v.rearrange("(o n) -> o n", o=1))

        r_all = const.tile([P, 2, 4], F32, name="r_all")

        def load_r():
            nc.sync.dma_start(out=r_sb[:], in_=r.rearrange("(g p t) -> p g t", g=2, p=P, t=4))

        def r_times():
            nc.vector.tensor_scalar(out=r_all[:], in0=r_sb[:], scalar1=float(D), scalar2=None, op0=ALU.mult)

        c1_codes = {}
        c1_scales = {}
        c1_grp = {}
        plan_codes = {}
        plan_scales = {}
        plan_grp = {}
        c2_codes = {}
        c2_scales = {}
        c2_grp = {}
        y_codes = {}
        y_scales = {}
        y_grp = {}
        y_bank = {}
        tr_bank = {}
        d2 = {}
        o_t = {}
        g_bank = {}
        x_t = {}
        e_t = {}
        nmax_t = {}
        total_t = {}
        rec_t = {}
        fac_t = {}
        ob_t = {}
        w_t = {}
        s_t = {}
        for jh in range(2):
            for mg in range(2):
                c2_codes[jh, mg] = codes.tile([P, 512], U32, name="c2_codes%d%d" % (jh, mg), align_bytes=64)
                c2_scales[jh, mg] = codes.tile([P, 512], U8, name="c2_scales%d%d" % (jh, mg), align_bytes=64)

        def quant(out_codes, out_scales, in_):
            nc.vector.quantize_mx(out=out_codes.bitcast(FP8X4), scales=out_scales, in_=in_)

        def copy_on(eng, out, in_):
            if eng == "S":
                nc.scalar.copy(out=out, in_=in_)
            elif eng == "V":
                nc.vector.tensor_copy(out=out, in_=in_)
            else:
                nc.gpsimd.tensor_scalar(out=out, in0=in_, scalar1=1.0, scalar2=0.0, op0=ALU.mult, op1=ALU.add)

        def turn(bank, words):
            for q in range(2):
                for u in range(2):
                    nc.tensor.transpose(bank[:, 2 * q + u, :], words[:, 256 * q + u : 256 * (q + 1) : 2], ident[:])

        def a_tr(k):
            tr_bank[k] = psum.tile([P, 4, P], F32, name="tr_bank", tag="bank")
            turn(tr_bank[k], c1_raw[k].bitcast(F32))

        def a_cp(k, eng):
            c1_grp[k] = work.tile([P, 2, P, 4], BF16, name="c1_grp", tag="c1_grp", bufs=4, align_bytes=64)
            copy_on(
                eng,
                c1_grp[k][:].rearrange("p q r t -> p (q r t)").bitcast(F32).rearrange("p (q r u) -> p q r u", q=2, u=2),
                tr_bank[k][:].rearrange("p (q u) r -> p q r u", q=2),
            )

        def a_q(k):
            c1_codes[k] = codes.tile([P, 2, P], U32, name="c1_codes%d" % k, align_bytes=64)
            c1_scales[k] = codes.tile([P, 2, P], U8, name="c1_scales%d" % k, align_bytes=64)
            quant(
                c1_codes[k][:].rearrange("p q r -> p (q r)"),
                c1_scales[k][:].rearrange("p q r -> p (q r)"),
                c1_grp[k][:].rearrange("p q r t -> p (q r t)"),
            )

        def p_cp(mg, q, eng):
            plan_grp[mg, q] = work.tile([P, 2048], BF16, name="plan_grp", tag="plan_grp", bufs=3, align_bytes=64)
            copy_on(
                eng,
                plan_grp[mg, q][:].rearrange("p (t m j) -> p m j t", t=4, j=4),
                plan_raw[mg, q].rearrange("p j (m t) -> p m j t", t=4),
            )

        def p_q(mg, q):
            plan_codes[mg, q] = codes.tile([P, 512], U32, name="plan_codes%d%d" % (mg, q), align_bytes=64)
            plan_scales[mg, q] = codes.tile([P, 512], U8, name="plan_scales%d%d" % (mg, q), align_bytes=64)
            quant(plan_codes[mg, q][:], plan_scales[mg, q][:], plan_grp[mg, q][:])

        def b_mm(k, mg):
            y_bank[k, mg] = psum.tile([P, 4, P], F32, name="y_bank", tag="bank")
            for t in range(4):
                for q in range(2):
                    nc.tensor.matmul_mx(
                        out=y_bank[k, mg][:, t, :],
                        lhsT=plan_codes[mg, q][:, P * t : P * t + P].bitcast(FP8X4),
                        lhsT_scale=plan_scales[mg, q][:, P * t : P * t + P],
                        rhs=c1_codes[k][:, q, :].bitcast(FP8X4),
                        rhs_scale=c1_scales[k][:, q, :],
                        start=(q == 0),
                        stop=(q == 1),
                    )

        def b_cp(k, mg, eng):
            if k not in y_grp:
                y_grp[k] = work.tile([P, 2, P, 4], BF16, name="y_grp", tag="y_grp", bufs=3, align_bytes=64)
            copy_on(eng, y_grp[k][:, mg, :, :], y_bank[k, mg][:].rearrange("p t n -> p n t"))

        def b_q(k):
            y_codes[k] = codes.tile([P, 2, P], U32, name="y_codes%d" % k, align_bytes=64)
            y_scales[k] = codes.tile([P, 2, P], U8, name="y_scales%d" % k, align_bytes=64)
            quant(
                y_codes[k][:].rearrange("p q r -> p (q r)"),
                y_scales[k][:].rearrange("p q r -> p (q r)"),
                y_grp[k][:].rearrange("p q r t -> p (q r t)"),
            )

        def e_tr(c, q):
            tr_bank["c2", c, q] = psum.tile([P, 2, 2, P], F32, name="c2_bank", tag="bank")
            for h in range(2):
                words = c2_raw[c][:, h, :].bitcast(F32)
                for u in range(2):
                    nc.tensor.transpose(
                        tr_bank["c2", c, q][:, h, u, :], words[:, 256 * q + u : 256 * (q + 1) : 2], ident[:]
                    )

        def e_cp(c, q, eng):
            c2_grp[c, q] = work.tile([P, 1024], BF16, name="c2_grp", tag="c2_grp", bufs=4, align_bytes=64)
            copy_on(
                eng,
                c2_grp[c, q][:].bitcast(F32).rearrange("p (r h u) -> p r h u", h=2, u=2),
                tr_bank["c2", c, q][:].rearrange("p h u r -> p r h u"),
            )

        def e_q(c, q):
            cols = slice(256 * (c % 2), 256 * (c % 2) + 256)
            quant(c2_codes[c // 2, q][:, cols], c2_scales[c // 2, q][:, cols], c2_grp[c, q][:])

        v2 = const.tile([P, D], BF16, name="v2")

        v_bank = {}

        def v_mm(jh):
            v_bank[jh] = psum.tile([P, 512], F32, name="v_bank", tag="bank")
            nc.tensor.matmul(v_bank[jh][:], lhsT=twos[:], rhs=vrow[:, 512 * jh : 512 * jh + 512], start=True, stop=True)

        def v_cp(jh, eng):
            copy_on(eng, v2[:, 512 * jh : 512 * jh + 512], v_bank[jh][:])

        def d_tt(k, jh, eng):
            d2[k, jh] = work.tile([P, 512], F32, name="d2", tag="d2_%d" % jh, bufs=1)
            cols = slice(512 * jh, 512 * jh + 512)
            engine = nc.gpsimd if eng == "G" else nc.vector
            engine.tensor_tensor(out=d2[k, jh][:], in0=v2[:, cols], in1=cost_raw[k][:, cols], op=ALU.subtract)

        def c_mm(k, jh):
            g_bank[k, jh] = psum.tile([P, 512], F32, name="g_bank", tag="bank")
            for mg in range(2):
                nc.tensor.matmul_mx(
                    out=g_bank[k, jh][:],
                    lhsT=y_codes[k][:, mg, :].bitcast(FP8X4),
                    lhsT_scale=y_scales[k][:, mg, :],
                    rhs=c2_codes[jh, mg][:].bitcast(FP8X4),
                    rhs_scale=c2_scales[jh, mg][:],
                    start=(mg == 0),
                    stop=(mg == 1),
                )

        def c_x(k, jh):
            if k not in x_t:
                x_t[k] = work.tile([P, D], F32, name="x", tag="x", bufs=3)
            cols = slice(512 * jh, 512 * jh + 512)
            nc.vector.scalar_tensor_tensor(
                out=x_t[k][:, cols], in0=d2[k, jh][:], scalar=0.5, in1=g_bank[k, jh][:], op0=ALU.mult, op1=ALU.add
            )

        def c_max(k):
            nmax_t[k] = work.tile([P, 1], F32, name="nmax", tag="nmax", bufs=3)
            nc.vector.tensor_reduce(out=nmax_t[k][:], in_=x_t[k][:], axis=AX.X, op=ALU.max, negate=True)

        def c_exp(k):
            e_t[k] = work.tile([P, D], F32, name="e", tag="e", bufs=3)
            total_t[k] = work.tile([P, 1], F32, name="total", tag="total", bufs=3)
            nc.scalar.activation(
                out=e_t[k][:], in_=x_t[k][:], func=ACT.Exp, bias=nmax_t[k][:], scale=1.0, accum_out=total_t[k][:]
            )

        def c_rec(k):
            rec_t[k] = work.tile([P, 1], F32, name="rec", tag="rec", bufs=3)
            nc.vector.reciprocal(rec_t[k][:], total_t[k][:])

        def c_fac(k):
            fac_t[k] = work.tile([P, 1], F32, name="fac", tag="fac", bufs=3)
            nc.vector.tensor_scalar(
                out=fac_t[k][:],
                in0=rec_t[k][:],
                scalar1=r_all[:, k // 4, k % 4 : k % 4 + 1],
                scalar2=None,
                op0=ALU.mult,
            )

        def c_sc(k, eng):
            g, t = k // 4, k % 4
            if g not in o_t:
                o_t[g] = work.tile([P, 4, D], F32, name="o_t", tag="o_t", bufs=2)
            if eng == "G":
                nc.gpsimd.tensor_scalar(
                    out=o_t[g][:, t, :],
                    in0=e_t[k][:],
                    scalar1=rec_t[k][:],
                    scalar2=r_all[:, g, t : t + 1],
                    op0=ALU.mult,
                    op1=ALU.mult,
                )
            elif eng == "S":
                nc.scalar.activation(out=o_t[g][:, t, :], in_=e_t[k][:], func=ACT.Copy, scale=fac_t[k][:])
            else:
                nc.vector.tensor_scalar(
                    out=o_t[g][:, t, :],
                    in0=e_t[k][:],
                    scalar1=rec_t[k][:],
                    scalar2=r_all[:, g, t : t + 1],
                    op0=ALU.mult,
                    op1=ALU.mult,
                )

        def c_sc_half(k, h):
            g, t = k // 4, k % 4
            cols = slice(512 * h, 512 * h + 512)
            nc.vector.tensor_scalar(
                out=o_t[g][:, t, cols],
                in0=e_t[k][:, cols],
                scalar1=rec_t[k][:],
                scalar2=r_all[:, g, t : t + 1],
                op0=ALU.mult,
                op1=ALU.mult,
            )

        def c_store(k):
            g, t = k // 4, k % 4
            nc.sync.dma_start(out=outv[g, t, :, :], in_=o_t[g][:, t, :])

        def f_cp(g, lo, hi, eng):
            if g not in ob_t:
                ob_t[g] = raw.tile([P, D, 4], BF16, name="ob", tag="plan_ob", bufs=2, align_bytes=64)
            if eng == "G":
                copy_on(eng, ob_t[g][:, lo:hi, :], o_t[g][:, :, lo:hi].rearrange("p t n -> p n t"))
            else:
                copy_on(
                    eng,
                    ob_t[g][:, lo:hi, :].rearrange("p (n i) t -> p n t i", i=4),
                    o_t[g][:, :, lo:hi].rearrange("p t (n i) -> p n t i", i=4),
                )

        def f_q(g, h):
            if g not in w_t:
                w_t[g] = work.tile([P, D], U32, name="w", tag="w", bufs=2, align_bytes=64)
                s_t[g] = work.tile([P, D], U8, name="s", tag="s", bufs=2, align_bytes=64)
            cols = slice(512 * h, 512 * h + 512)
            quant(w_t[g][:, cols], s_t[g][:, cols], ob_t[g][:, cols, :].rearrange("p n t -> p (n t)"))

        def f_store(g, cols):
            nc.sync.dma_start(
                out=words_out[g, :, cols, :].rearrange("p n t -> p (n t)").bitcast(I32),
                in_=w_t[g][:, cols].bitcast(I32),
            )

        def f_s(g):
            for a in range(4):
                nc.sync.dma_start(
                    out=scales_out[g, 4 * a : 4 * a + 4, :].bitcast(I32), in_=s_t[g][32 * a : 32 * a + 4, :].bitcast(I32)
                )


        load_c1(0)
        a_tr(0)
        load_c2(0)
        load_plan(1, None)
        a_cp(0, "V")
        e_tr(0, 0)
        e_tr(0, 1)
        load_c1(1)
        load_c1(2)
        a_tr(1)
        e_cp(0, 0, "S")
        a_q(0)
        e_q(0, 0)
        e_cp(0, 1, "V")
        p_cp(0, 1, "S")
        a_cp(1, "S")
        a_tr(2)
        a_cp(2, "S")
        p_cp(1, 1, "V")
        p_q(1, 1)
        a_tr(3)
        a_cp(3, "S")
        p_q(0, 1)
        load_v()
        v_mm(0)
        v_mm(1)
        load_plan(0, 0)
        v_cp(0, "S")
        v_cp(1, "S")
        a_q(1)
        p_cp(0, 0, "V")
        load_c2(3)
        e_tr(3, 1)
        e_cp(3, 1, "S")
        e_tr(3, 0)
        a_q(3)
        load_plan(0, 1)
        load_c1(3)
        p_q(0, 0)
        b_mm(0, 0)
        a_q(2)
        e_cp(3, 0, "S")
        load_c2(2)
        e_q(0, 1)
        p_cp(1, 0, "V")
        b_mm(3, 0)
        a_tr(5)
        e_q(3, 1)
        a_tr(4)
        b_cp(3, 0, "S")
        e_tr(2, 1)
        load_c2(1)
        a_cp(5, "S")
        p_q(1, 0)
        a_cp(4, "S")
        e_q(3, 0)
        load_cost(1)
        e_cp(2, 1, "S")
        b_mm(3, 1)
        b_cp(0, 0, "V")
        a_q(5)
        a_q(4)
        e_tr(2, 0)
        e_q(2, 1)
        load_r()
        d_tt(3, 1, "V")
        b_cp(3, 1, "S")
        b_q(3)
        e_cp(2, 0, "S")
        e_q(2, 0)
        d_tt(3, 0, "V")
        e_tr(1, 1)
        e_cp(1, 1, "S")
        e_q(1, 1)
        e_tr(1, 0)
        e_cp(1, 0, "S")
        e_q(1, 0)
        b_mm(0, 1)
        b_cp(0, 1, "S")
        c_mm(3, 1)
        c_x(3, 1)
        b_mm(1, 0)
        c_mm(3, 0)
        b_cp(1, 0, "S")
        b_mm(2, 1)
        b_cp(2, 1, "S")
        b_mm(2, 0)
        b_cp(2, 0, "S")
        load_c1(4)
        b_q(0)
        load_cost(0)
        c_x(3, 0)
        c_max(3)
        c_mm(0, 1)
        c_mm(0, 0)
        c_exp(3)
        b_mm(1, 1)
        b_cp(1, 1, "S")
        a_tr(6)
        a_cp(6, "S")
        a_tr(7)
        d_tt(0, 1, "G")
        c_x(0, 1)
        d_tt(0, 0, "G")
        d_tt(2, 1, "G")
        b_q(2)
        c_mm(2, 0)
        c_x(0, 0)
        r_times()
        c_rec(3)
        c_fac(3)
        c_max(0)
        b_mm(5, 1)
        b_q(1)
        a_cp(7, "S")
        load_cost(2)
        a_q(7)
        c_sc(3, "S")
        d_tt(2, 0, "G")
        b_mm(5, 0)
        d_tt(1, 0, "G")
        a_q(6)
        c_x(2, 0)
        b_cp(5, 1, "S")
        c_exp(0)
        c_mm(2, 1)
        c_x(2, 1)
        c_mm(1, 0)
        c_max(2)
        c_x(1, 0)
        c_mm(1, 1)
        b_cp(5, 0, "S")
        load_cost(3)
        b_q(5)
        b_mm(6, 0)
        b_cp(6, 0, "S")
        d_tt(1, 1, "G")
        b_mm(4, 0)
        c_x(1, 1)
        c_rec(0)
        b_cp(4, 0, "S")
        b_mm(6, 1)
        b_cp(6, 1, "S")
        b_mm(4, 1)
        c_exp(2)
        b_cp(4, 1, "S")
        c_mm(5, 0)
        c_max(1)
        c_exp(1)
        d_tt(5, 0, "G")
        c_x(5, 0)
        b_q(6)
        c_fac(0)
        b_mm(7, 0)
        b_cp(7, 0, "S")
        c_rec(2)
        d_tt(5, 1, "G")
        c_mm(5, 1)
        c_x(5, 1)
        d_tt(6, 0, "G")
        b_mm(7, 1)
        c_rec(1)
        c_store(3)
        c_sc(0, "S")
        c_store(0)
        c_max(5)
        c_fac(1)
        c_sc(1, "S")
        c_mm(6, 0)
        c_x(6, 0)
        c_store(1)
        c_exp(5)
        c_mm(6, 1)
        d_tt(6, 1, "G")
        c_x(6, 1)
        c_sc(2, "G")
        f_cp(0, 768, 1024, "S")
        b_q(4)
        c_mm(4, 1)
        d_tt(4, 1, "G")
        d_tt(4, 0, "G")
        b_cp(7, 1, "V")
        c_store(2)
        c_max(6)
        c_exp(6)
        c_x(4, 1)
        b_q(7)
        c_mm(4, 0)
        c_x(4, 0)
        c_rec(5)
        d_tt(7, 1, "G")
        f_cp(0, 512, 768, "S")
        f_cp(0, 0, 256, "S")
        c_max(4)
        c_mm(7, 1)
        d_tt(7, 0, "G")
        c_x(7, 1)
        c_mm(7, 0)
        c_x(7, 0)
        c_rec(6)
        c_exp(4)
        c_sc(5, "G")
        c_max(7)
        c_exp(7)
        c_sc(6, "G")
        c_rec(4)
        f_q(0, 1)
        c_store(5)
        c_store(6)
        f_cp(0, 256, 512, "S")
        c_sc(4, "V")
        f_store(0, slice(512, 1024))
        c_rec(7)
        c_sc_half(7, 0)
        c_sc_half(7, 1)
        f_cp(1, 256, 512, "V")
        c_store(4)
        c_store(7)
        f_cp(1, 512, 640, "S")
        f_cp(1, 0, 256, "V")
        f_q(0, 0)
        f_store(0, slice(0, 512))
        f_s(0)
        f_q(1, 0)
        f_cp(1, 640, 1024, "S")
        f_store(1, slice(0, 512))
        f_q(1, 1)
        f_store(1, slice(512, 1024))
        f_s(1)
